import numpy as np
import ml_dtypes


def mxq(x, axis, fmt="e4m3"):
    dtype, down = {"e4m3": (ml_dtypes.float8_e4m3fn, 7), "e5m2": (ml_dtypes.float8_e5m2, 14)}[fmt]
    v = np.moveaxis(np.asarray(x, np.float32).astype(ml_dtypes.bfloat16).astype(np.float64), axis, -1)
    blocks = v.reshape(v.shape[:-1] + (-1, 32))
    amax = np.abs(blocks).max(-1, keepdims=True)
    byte = np.maximum(np.where(amax > 0, np.frexp(amax)[1] - 1 + 127, 0) - down, 1)
    scale = np.exp2(byte - 127.0)
    codes = (blocks / scale).astype(np.float32).astype(dtype).astype(np.float64)
    return np.moveaxis((codes * scale).reshape(v.shape), -1, axis)


WIDE = False


def mx_kscale(k):
    if not WIDE:
        return np.ones(k)
    levels = np.array([30, -30])
    if k % 512:
        return np.exp2(np.random.permutation(np.resize(levels, k // 32))).repeat(32)
    a = np.empty((k // 512, 16))
    for p in range(k // 512):
        a[p, :8] = np.random.permutation(np.resize(levels, 8))
        for g in range(8):
            far = levels[np.abs(levels - a[p, g]) >= 10]
            a[p, g + 8] = far[np.random.randint(len(far))]
    return np.exp2(a.ravel()).repeat(32)


def f64(x):
    return np.asarray(x).astype(np.float64)


def striped(idx):
    return np.tile(np.asarray(idx).reshape(-1, 16).T, (8, 1)).astype(np.uint16)


def unstriped(offs):
    return offs[:16].T.reshape(-1).astype(np.int64)


def bf(x):
    return np.asarray(x, np.float32).astype(ml_dtypes.bfloat16)


def planes(Y):
    r, m = Y.shape
    b = f64(bf(Y)).reshape(r // 32, 32, m)
    amax = np.abs(b).max(1)
    byte = np.clip(np.where(amax > 0, np.frexp(amax)[1] - 1 + 127 - 7, 1), 1, 254)
    codes = (b * np.exp2(127.0 - byte)[:, None, :]).reshape(r, m).astype(np.float32).astype(ml_dtypes.float8_e4m3fn).view(np.uint8)
    words = codes.reshape(r // 512, 128, 4, m).transpose(0, 1, 3, 2)
    return np.ascontiguousarray(words), np.ascontiguousarray(byte.astype(np.uint8).reshape(r // 512, 16, m))


K, N, T, S, J, I = 512, 512, 1024, 1024, 512, 512


def setup_inputs():
    n = np.random.standard_normal
    idx = np.random.permutation(T)[:J]
    idx2 = np.random.permutation(S)[:I]
    fj = mx_kscale(J)
    fi = mx_kscale(I)
    tj = np.ones(T)
    tj[idx] = fj
    ti = np.ones(S)
    ti[idx2] = fi
    return {
        "xa": (n((K, T)) * tj).astype(np.float32),
        "ga": (n((N, T)) * np.exp(0.5 * n((1, T))) / tj).astype(np.float32),
        "xb": (n((K, S)) * ti).astype(np.float32),
        "gb": (n((N, S)) / ti).astype(np.float32),
        "offs": striped(idx),
        "offs2": striped(idx2),
    }


def reference(xa, ga, xb, gb, offs, offs2):
    idx = unstriped(offs)
    idx2 = unstriped(offs2)
    x1 = f64(xa)[:, idx].T
    g1 = f64(ga)[:, idx].T
    x2 = f64(xb)[:, idx2].T
    g2 = f64(gb)[:, idx2].T
    x1q = mxq(x1, 0, "e4m3")
    g1q = mxq(g1, 0, "e5m2")
    x2q = mxq(x2, 0, "e4m3")
    g2q = mxq(g2, 0, "e4m3")
    w = x1q.T @ g1q + x2q.T @ g2q
    y = 0.04 * w
    words, scales = planes(y)
    return y, words, scales

@@ -1,0 +1,180 @@
+from contextlib import ExitStack
+
+import concourse.mybir as mybir
+from concourse.masks import make_identity
+
+F32 = mybir.dt.float32
+BF16 = mybir.dt.bfloat16
+I32 = mybir.dt.int32
+U32 = mybir.dt.uint32
+U16 = mybir.dt.uint16
+U8 = mybir.dt.uint8
+E4M3 = mybir.dt.float8_e4m3fn_x4
+E5M2 = mybir.dt.float8_e5m2_x4
+COPY = mybir.ActivationFunctionType.Copy
+MULT = mybir.AluOpType.mult
+
+P = 128
+PACK = 4
+TOKENS = 1024
+LISTED = 512
+LIST_COLS = LISTED // 16
+BLOCKS = 4
+AHEAD = 4
+FACTOR = 0.04
+VECTOR_COLS_X = 4
+VECTOR_COLS_G = 6
+VECTOR_COLS_LAST = 16
+WINDOW_BYTES = 4 * TOKENS
+GROUPED_BYTES = 2 * LISTED
+
+FLOPS = 2 * 2 * 512 * 512 * 512
+
+
+def tile_list_wgrad_two_batches_pl_kernel(tc, xa, ga, xb, gb, offs, offs2, out_0, out_1, out_2):
+    nc = tc.nc
+    with ExitStack() as ctx:
+        keep = ctx.enter_context(tc.tile_pool(name="keep", bufs=1))
+        ring = ctx.enter_context(tc.tile_pool(name="ring", bufs=4))
+        laid = ctx.enter_context(tc.tile_pool(name="laid", bufs=1))
+        turn_psum = ctx.enter_context(tc.psum_pool(name="turn_psum", bufs=4))
+        sum_psum = ctx.enter_context(tc.psum_pool(name="sum_psum", bufs=2))
+
+        list_a = keep.tile([P, LIST_COLS], U16, name="list_a")
+        list_b = keep.tile([P, LIST_COLS], U16, name="list_b")
+        identity = keep.tile([P, P], F32, name="identity")
+        make_identity(nc, identity[:])
+
+        xa_rows = xa.rearrange("(m t) c -> t m c", t=PACK)
+        xb_rows = xb.rearrange("(m t) c -> t m c", t=PACK)
+        steps = []
+        for t in range(PACK):
+            steps.append((xa_rows[t], list_a, E4M3))
+            steps.append((xb_rows[t], list_b, E4M3))
+        for b in range(BLOCKS):
+            steps.append((ga[b * P : (b + 1) * P, :], list_a, E5M2))
+            steps.append((gb[b * P : (b + 1) * P, :], list_b, E4M3))
+        n_steps = len(steps)
+        last_step = n_steps - 1
+
+        windows = []
+        for s in range(n_steps):
+            window = laid.tile([P, TOKENS], F32, name="window%d" % s, offset=s * WINDOW_BYTES, align_bytes=64)
+            nc.sync.dma_start(window[:], steps[s][0])
+            windows.append(window)
+            if s == 0:
+                nc.sync.dma_start(list_a[:], offs)
+                nc.sync.dma_start(list_b[:], offs2)
+
+        scales = [keep.tile([P, P], U8, name="scales%d" % s, align_bytes=64) for s in range(n_steps)]
+        y_codes = keep.tile([P, BLOCKS * P], U32, name="y_codes", align_bytes=64)
+        y_scales = keep.tile([P, BLOCKS * P], U8, name="y_scales", align_bytes=64)
+        y_rows = out_0.rearrange("(p t) n -> p t n", t=PACK)
+        word_rows = out_1[0].rearrange("p n t -> p (n t)").bitcast(I32)
+        scale_rows = out_2[0].bitcast(I32)
+
+        turned = {}
+        grouped = {}
+        codes = {}
+        sums = {}
+        ys = {}
+        rounded = {}
+
+        def gather_and_turn(s):
+            picked = ring.tile([P, LISTED], BF16, name="picked", align_bytes=64)
+            offsets = steps[s][1]
+            share = VECTOR_COLS_LAST if s == last_step else VECTOR_COLS_X if s < 2 * PACK else VECTOR_COLS_G
+            nc.vector.tensor_copy(picked[:, : 16 * share], windows[s][:].indirect(offsets[:, :share]))
+            nc.scalar.activation(picked[:, 16 * share :], windows[s][:].indirect(offsets[:, share:]), COPY)
+            pairs = picked[:].bitcast(F32)
+            bank = turn_psum.tile([P, 2, P], F32, name="bank")
+            for u in range(2):
+                nc.tensor.transpose(bank[:, u, :], pairs[:, u::2], identity[:])
+            turned[s] = bank
+
+        def regroup(s):
+            grouped[s] = ring.tile([P, P * PACK], BF16, name="grouped", align_bytes=64)
+            copy = nc.scalar.copy if s >= last_step - 1 else nc.vector.tensor_copy
+            copy(
+                grouped[s][:].bitcast(F32).rearrange("p (r u) -> p r u", u=2),
+                turned[s][:].rearrange("p u r -> p r u"),
+            )
+
+        def quantise(s):
+            if s == last_step - 2:
+                at = last_step * WINDOW_BYTES
+                codes[s] = laid.tile([P, P], U32, name="codes%d" % s, offset=at, align_bytes=64)
+            else:
+                codes[s] = keep.tile([P, P], U32, name="codes%d" % s, align_bytes=64)
+            nc.vector.quantize_mx(codes[s][:].bitcast(steps[s][2]), scales[s][:], grouped[s][:])
+
+        def multiply(s):
+            b, batch = divmod(s - 2 * PACK, 2)
+            if batch == 0:
+                sums[b] = [sum_psum.tile([P, 2, P], F32, name="sum%d" % h) for h in range(2)]
+            for t in range(PACK):
+                x = 2 * t + batch
+                nc.tensor.matmul_mx(
+                    sums[b][t // 2][:, t % 2, :],
+                    lhsT=codes[x][:].bitcast(E4M3),
+                    lhsT_scale=scales[x][:],
+                    rhs=codes[s][:].bitcast(steps[s][2]),
+                    rhs_scale=scales[s][:],
+                    start=(batch == 0 and t % 2 == 0),
+                    stop=(batch == 1 and t % 2 == 1),
+                )
+
+        def scale_out(b, h):
+            if h == 0:
+                if b == 1:
+                    at = last_step * WINDOW_BYTES + GROUPED_BYTES
+                    ys[b] = laid.tile([P, PACK, P], F32, name="y%d" % b, offset=at, align_bytes=64)
+                else:
+                    ys[b] = keep.tile([P, PACK, P], F32, name="y%d" % b, align_bytes=64)
+            half = ys[b][:, 2 * h : 2 * h + 2, :]
+            if h == 1 or b == 0:
+                nc.vector.tensor_scalar(half, sums[b][h][:], FACTOR, None, MULT)
+            else:
+                nc.scalar.activation(half, sums[b][h][:], COPY, scale=FACTOR)
+            if h == 1:
+                nc.sync.dma_start(y_rows[:, :, b * P : (b + 1) * P], ys[b][:])
+
+        def round_result(b):
+            rounded[b] = keep.tile([P, P * PACK], BF16, name="rounded%d" % b, align_bytes=64)
+            copy = nc.scalar.copy if b == BLOCKS - 2 else nc.vector.tensor_copy
+            copy(
+                rounded[b][:].rearrange("p (c i t) -> p c t i", i=4, t=PACK),
+                ys[b][:].rearrange("p t (c i) -> p c t i", i=4),
+            )
+
+        def quantise_result(b):
+            cols = slice(b * P, (b + 1) * P)
+            nc.vector.quantize_mx(y_codes[:, cols].bitcast(E4M3), y_scales[:, cols], rounded[b][:])
+            if b == BLOCKS - 2:
+                nc.sync.dma_start(word_rows[:, : (b + 1) * P], y_codes[:, : (b + 1) * P].bitcast(I32))
+
+        for s in range(AHEAD):
+            gather_and_turn(s)
+        for s in range(n_steps):
+            done = s // 2 - PACK - 1
+            regroup(s)
+            quantise(s)
+            if s >= 2 * PACK:
+                multiply(s)
+            if s + AHEAD < n_steps:
+                gather_and_turn(s + AHEAD)
+            if done >= 0 and s % 2 == 0:
+                scale_out(done, 0)
+                scale_out(done, 1)
+            if done >= 0 and s % 2 == 1:
+                round_result(done)
+                quantise_result(done)
+        scale_out(BLOCKS - 1, 0)
+        scale_out(BLOCKS - 1, 1)
+        round_result(BLOCKS - 1)
+        quantise_result(BLOCKS - 1)
+        last = slice((BLOCKS - 1) * P, BLOCKS * P)
+        nc.sync.dma_start(word_rows[:, last], y_codes[:, last].bitcast(I32))
+        for q in range(4):
+            queue = nc.scalar if q % 2 == 0 else nc.sync
+            queue.dma_start(scale_rows[4 * q : 4 * q + 4, :], y_scales[32 * q : 32 * q + 4, :].bitcast(I32))

@@ -22,9 +22,7 @@ LIST_COLS = LISTED // 16
 BLOCKS = 4
 AHEAD = 4
 FACTOR = 0.04
-VECTOR_COLS_X = 4
-VECTOR_COLS_G = 6
-VECTOR_COLS_LAST = 16
+VECTOR_COLS_X = 8
 WINDOW_BYTES = 4 * TOKENS
 GROUPED_BYTES = 2 * LISTED
 
@@ -35,7 +33,7 @@ def tile_list_wgrad_two_batches_pl_kernel(tc, xa, ga, xb, gb, offs, offs2, out_0
     nc = tc.nc
     with ExitStack() as ctx:
         keep = ctx.enter_context(tc.tile_pool(name="keep", bufs=1))
-        ring = ctx.enter_context(tc.tile_pool(name="ring", bufs=4))
+        ring = ctx.enter_context(tc.tile_pool(name="ring", bufs=6))
         laid = ctx.enter_context(tc.tile_pool(name="laid", bufs=1))
         turn_psum = ctx.enter_context(tc.psum_pool(name="turn_psum", bufs=4))
         sum_psum = ctx.enter_context(tc.psum_pool(name="sum_psum", bufs=2))
@@ -44,6 +42,10 @@ def tile_list_wgrad_two_batches_pl_kernel(tc, xa, ga, xb, gb, offs, offs2, out_0
         list_b = keep.tile([P, LIST_COLS], U16, name="list_b")
         identity = keep.tile([P, P], F32, name="identity")
         make_identity(nc, identity[:])
+        warm_in = keep.tile([P, 1], F32, name="warm_in")
+        warm_out = keep.tile([P, 1], F32, name="warm_out")
+        nc.vector.memset(warm_in[:], 0.0)
+        nc.scalar.activation(warm_out[:], warm_in[:], COPY)
 
         xa_rows = xa.rearrange("(m t) c -> t m c", t=PACK)
         xb_rows = xb.rearrange("(m t) c -> t m c", t=PACK)
@@ -83,9 +85,12 @@ def tile_list_wgrad_two_batches_pl_kernel(tc, xa, ga, xb, gb, offs, offs2, out_0
         def gather_and_turn(s):
             picked = ring.tile([P, LISTED], BF16, name="picked", align_bytes=64)
             offsets = steps[s][1]
-            share = VECTOR_COLS_LAST if s == last_step else VECTOR_COLS_X if s < 2 * PACK else VECTOR_COLS_G
-            nc.vector.tensor_copy(picked[:, : 16 * share], windows[s][:].indirect(offsets[:, :share]))
-            nc.scalar.activation(picked[:, 16 * share :], windows[s][:].indirect(offsets[:, share:]), COPY)
+            if s < 2 * PACK:
+                share = VECTOR_COLS_X
+                nc.vector.tensor_copy(picked[:, : 16 * share], windows[s][:].indirect(offsets[:, :share]))
+                nc.scalar.activation(picked[:, 16 * share :], windows[s][:].indirect(offsets[:, share:]), COPY)
+            else:
+                nc.scalar.activation(picked[:], windows[s][:].indirect(offsets[:]), COPY)
             pairs = picked[:].bitcast(F32)
             bank = turn_psum.tile([P, 2, P], F32, name="bank")
             for u in range(2):
@@ -93,16 +98,22 @@ def tile_list_wgrad_two_batches_pl_kernel(tc, xa, ga, xb, gb, offs, offs2, out_0
             turned[s] = bank
 
         def regroup(s):
-            grouped[s] = ring.tile([P, P * PACK], BF16, name="grouped", align_bytes=64)
-            copy = nc.scalar.copy if s >= last_step - 1 else nc.vector.tensor_copy
+            if s + 1 < 2 * PACK:
+                at = (s + 1) * WINDOW_BYTES
+                grouped[s] = laid.tile([P, P * PACK], BF16, name="grouped%d" % s, offset=at, align_bytes=64)
+            else:
+                grouped[s] = keep.tile([P, P * PACK], BF16, name="grouped%d" % s, align_bytes=64)
+            copy = nc.scalar.copy if s == last_step else nc.vector.tensor_copy
             copy(
                 grouped[s][:].bitcast(F32).rearrange("p (r u) -> p r u", u=2),
                 turned[s][:].rearrange("p u r -> p r u"),
             )
 
         def quantise(s):
-            if s == last_step - 2:
-                at = last_step * WINDOW_BYTES
+            if 2 * PACK <= s + 1 <= last_step:
+                at = (s + 1) * WINDOW_BYTES
+                if s == last_step - 2:
+                    at = last_step * WINDOW_BYTES + GROUPED_BYTES
                 codes[s] = laid.tile([P, P], U32, name="codes%d" % s, offset=at, align_bytes=64)
             else:
                 codes[s] = keep.tile([P, P], U32, name="codes%d" % s, align_bytes=64)
@@ -126,13 +137,9 @@ def tile_list_wgrad_two_batches_pl_kernel(tc, xa, ga, xb, gb, offs, offs2, out_0
 
         def scale_out(b, h):
             if h == 0:
-                if b == 1:
-                    at = last_step * WINDOW_BYTES + GROUPED_BYTES
-                    ys[b] = laid.tile([P, PACK, P], F32, name="y%d" % b, offset=at, align_bytes=64)
-                else:
-                    ys[b] = keep.tile([P, PACK, P], F32, name="y%d" % b, align_bytes=64)
+                ys[b] = keep.tile([P, PACK, P], F32, name="y%d" % b, align_bytes=64)
             half = ys[b][:, 2 * h : 2 * h + 2, :]
-            if h == 1 or b == 0:
+            if b < BLOCKS - 2 or (b == BLOCKS - 1 and h == 1):
                 nc.vector.tensor_scalar(half, sums[b][h][:], FACTOR, None, MULT)
             else:
                 nc.scalar.activation(half, sums[b][h][:], COPY, scale=FACTOR)
@@ -140,12 +147,18 @@ def tile_list_wgrad_two_batches_pl_kernel(tc, xa, ga, xb, gb, offs, offs2, out_0
                 nc.sync.dma_start(y_rows[:, :, b * P : (b + 1) * P], ys[b][:])
 
         def round_result(b):
-            rounded[b] = keep.tile([P, P * PACK], BF16, name="rounded%d" % b, align_bytes=64)
-            copy = nc.scalar.copy if b == BLOCKS - 2 else nc.vector.tensor_copy
-            copy(
-                rounded[b][:].rearrange("p (c i t) -> p c t i", i=4, t=PACK),
-                ys[b][:].rearrange("p t (c i) -> p c t i", i=4),
-            )
+            if b < BLOCKS - 2:
+                at = (2 * PACK + 2 * b + 4) * WINDOW_BYTES + GROUPED_BYTES
+                rounded[b] = laid.tile([P, P * PACK], BF16, name="rounded%d" % b, offset=at, align_bytes=64)
+            else:
+                rounded[b] = keep.tile([P, P * PACK], BF16, name="rounded%d" % b, align_bytes=64)
+            target = rounded[b][:].rearrange("p (c i t) -> p c t i", i=4, t=PACK)
+            source = ys[b][:].rearrange("p t (c i) -> p c t i", i=4)
+            if b < BLOCKS - 2:
+                nc.vector.tensor_copy(target, source)
+            else:
+                nc.vector.tensor_copy(target[:, :16], source[:, :16])
+                nc.scalar.copy(target[:, 16:], source[:, 16:])
 
         def quantise_result(b):
             cols = slice(b * P, (b + 1) * P)

@@ -42,10 +42,6 @@ def tile_list_wgrad_two_batches_pl_kernel(tc, xa, ga, xb, gb, offs, offs2, out_0
         list_b = keep.tile([P, LIST_COLS], U16, name="list_b")
         identity = keep.tile([P, P], F32, name="identity")
         make_identity(nc, identity[:])
-        warm_in = keep.tile([P, 1], F32, name="warm_in")
-        warm_out = keep.tile([P, 1], F32, name="warm_out")
-        nc.vector.memset(warm_in[:], 0.0)
-        nc.scalar.activation(warm_out[:], warm_in[:], COPY)
 
         xa_rows = xa.rearrange("(m t) c -> t m c", t=PACK)
         xb_rows = xb.rearrange("(m t) c -> t m c", t=PACK)

@@ -22,7 +22,7 @@ LIST_COLS = LISTED // 16
 BLOCKS = 4
 AHEAD = 4
 FACTOR = 0.04
-VECTOR_COLS_X = 8
+VECTOR_COLS_X = 16
 WINDOW_BYTES = 4 * TOKENS
 GROUPED_BYTES = 2 * LISTED
 
@@ -54,6 +54,7 @@ def tile_list_wgrad_two_batches_pl_kernel(tc, xa, ga, xb, gb, offs, offs2, out_0
             steps.append((gb[b * P : (b + 1) * P, :], list_b, E4M3))
         n_steps = len(steps)
         last_step = n_steps - 1
+        shared = list(range(1, last_step - 3, 2)) + [last_step - 1]
 
         windows = []
         for s in range(n_steps):
@@ -81,7 +82,7 @@ def tile_list_wgrad_two_batches_pl_kernel(tc, xa, ga, xb, gb, offs, offs2, out_0
         def gather_and_turn(s):
             picked = ring.tile([P, LISTED], BF16, name="picked", align_bytes=64)
             offsets = steps[s][1]
-            if s < 2 * PACK:
+            if s in shared:
                 share = VECTOR_COLS_X
                 nc.vector.tensor_copy(picked[:, : 16 * share], windows[s][:].indirect(offsets[:, :share]))
                 nc.scalar.activation(picked[:, 16 * share :], windows[s][:].indirect(offsets[:, share:]), COPY)
@@ -94,7 +95,7 @@ def tile_list_wgrad_two_batches_pl_kernel(tc, xa, ga, xb, gb, offs, offs2, out_0
             turned[s] = bank
 
         def regroup(s):
-            if s + 1 < 2 * PACK:
+            if s + 1 in shared:
                 at = (s + 1) * WINDOW_BYTES
                 grouped[s] = laid.tile([P, P * PACK], BF16, name="grouped%d" % s, offset=at, align_bytes=64)
             else:
@@ -106,10 +107,10 @@ def tile_list_wgrad_two_batches_pl_kernel(tc, xa, ga, xb, gb, offs, offs2, out_0
             )
 
         def quantise(s):
-            if 2 * PACK <= s + 1 <= last_step:
-                at = (s + 1) * WINDOW_BYTES
-                if s == last_step - 2:
-                    at = last_step * WINDOW_BYTES + GROUPED_BYTES
+            if s + 2 in shared or s in (last_step - 2, last_step - 1):
+                at = (s + 2) * WINDOW_BYTES + GROUPED_BYTES
+                if s == last_step - 1:
+                    at = last_step * WINDOW_BYTES
                 codes[s] = laid.tile([P, P], U32, name="codes%d" % s, offset=at, align_bytes=64)
             else:
                 codes[s] = keep.tile([P, P], U32, name="codes%d" % s, align_bytes=64)
@@ -133,9 +134,13 @@ def tile_list_wgrad_two_batches_pl_kernel(tc, xa, ga, xb, gb, offs, offs2, out_0
 
         def scale_out(b, h):
             if h == 0:
-                ys[b] = keep.tile([P, PACK, P], F32, name="y%d" % b, align_bytes=64)
+                if b == 1:
+                    at = last_step * WINDOW_BYTES + 2 * GROUPED_BYTES
+                    ys[b] = laid.tile([P, PACK, P], F32, name="y%d" % b, offset=at, align_bytes=64)
+                else:
+                    ys[b] = keep.tile([P, PACK, P], F32, name="y%d" % b, align_bytes=64)
             half = ys[b][:, 2 * h : 2 * h + 2, :]
-            if b < BLOCKS - 2 or (b == BLOCKS - 1 and h == 1):
+            if b == 0 or (b == BLOCKS - 1 and h == 1):
                 nc.vector.tensor_scalar(half, sums[b][h][:], FACTOR, None, MULT)
             else:
                 nc.scalar.activation(half, sums[b][h][:], COPY, scale=FACTOR)
@@ -143,11 +148,7 @@ def tile_list_wgrad_two_batches_pl_kernel(tc, xa, ga, xb, gb, offs, offs2, out_0
                 nc.sync.dma_start(y_rows[:, :, b * P : (b + 1) * P], ys[b][:])
 
         def round_result(b):
-            if b < BLOCKS - 2:
-                at = (2 * PACK + 2 * b + 4) * WINDOW_BYTES + GROUPED_BYTES
-                rounded[b] = laid.tile([P, P * PACK], BF16, name="rounded%d" % b, offset=at, align_bytes=64)
-            else:
-                rounded[b] = keep.tile([P, P * PACK], BF16, name="rounded%d" % b, align_bytes=64)
+            rounded[b] = keep.tile([P, P * PACK], BF16, name="rounded%d" % b, align_bytes=64)
             target = rounded[b][:].rearrange("p (c i t) -> p c t i", i=4, t=PACK)
             source = ys[b][:].rearrange("p t (c i) -> p c t i", i=4)
             if b < BLOCKS - 2:

@@ -18,13 +18,19 @@ P = 128
 PACK = 4
 TOKENS = 1024
 LISTED = 512
-LIST_COLS = LISTED // 16
+ENTRIES_PER_COL = 16
+LIST_COLS = LISTED // ENTRIES_PER_COL
 BLOCKS = 4
-AHEAD = 4
+QUADRANTS = 4
 FACTOR = 0.04
-VECTOR_COLS_X = 16
+X_STEPS = 2 * PACK
+AHEAD = 4
+PICKED_BUFS = 6
+SUM_BUFS = 2
+VECTOR_LIST_COLS = LIST_COLS // 2
+EARLY_WORD_BLOCKS = 2
 WINDOW_BYTES = 4 * TOKENS
-GROUPED_BYTES = 2 * LISTED
+SLOT_BYTES = 2 * LISTED
 
 FLOPS = 2 * 2 * 512 * 512 * 512
 
@@ -33,10 +39,14 @@ def tile_list_wgrad_two_batches_pl_kernel(tc, xa, ga, xb, gb, offs, offs2, out_0
     nc = tc.nc
     with ExitStack() as ctx:
         keep = ctx.enter_context(tc.tile_pool(name="keep", bufs=1))
-        ring = ctx.enter_context(tc.tile_pool(name="ring", bufs=6))
+        ring = ctx.enter_context(tc.tile_pool(name="ring", bufs=PICKED_BUFS))
         laid = ctx.enter_context(tc.tile_pool(name="laid", bufs=1))
-        turn_psum = ctx.enter_context(tc.psum_pool(name="turn_psum", bufs=4))
-        sum_psum = ctx.enter_context(tc.psum_pool(name="sum_psum", bufs=2))
+        turn_psum = ctx.enter_context(tc.psum_pool(name="turn_psum", bufs=AHEAD))
+        sum_psum = ctx.enter_context(tc.psum_pool(name="sum_psum", bufs=SUM_BUFS))
+
+        def over_window(s, slot, shape, dtype, name):
+            at = s * WINDOW_BYTES + slot * SLOT_BYTES
+            return laid.tile(shape, dtype, name=name, offset=at, align_bytes=64)
 
         list_a = keep.tile([P, LIST_COLS], U16, name="list_a")
         list_b = keep.tile([P, LIST_COLS], U16, name="list_b")
@@ -54,11 +64,12 @@ def tile_list_wgrad_two_batches_pl_kernel(tc, xa, ga, xb, gb, offs, offs2, out_0
             steps.append((gb[b * P : (b + 1) * P, :], list_b, E4M3))
         n_steps = len(steps)
         last_step = n_steps - 1
+        last_block = BLOCKS - 1
         shared = list(range(1, last_step - 3, 2)) + [last_step - 1]
 
         windows = []
         for s in range(n_steps):
-            window = laid.tile([P, TOKENS], F32, name="window%d" % s, offset=s * WINDOW_BYTES, align_bytes=64)
+            window = over_window(s, 0, [P, TOKENS], F32, "window%d" % s)
             nc.sync.dma_start(window[:], steps[s][0])
             windows.append(window)
             if s == 0:
@@ -83,9 +94,9 @@ def tile_list_wgrad_two_batches_pl_kernel(tc, xa, ga, xb, gb, offs, offs2, out_0
             picked = ring.tile([P, LISTED], BF16, name="picked", align_bytes=64)
             offsets = steps[s][1]
             if s in shared:
-                share = VECTOR_COLS_X
-                nc.vector.tensor_copy(picked[:, : 16 * share], windows[s][:].indirect(offsets[:, :share]))
-                nc.scalar.activation(picked[:, 16 * share :], windows[s][:].indirect(offsets[:, share:]), COPY)
+                split = ENTRIES_PER_COL * VECTOR_LIST_COLS
+                nc.vector.tensor_copy(picked[:, :split], windows[s][:].indirect(offsets[:, :VECTOR_LIST_COLS]))
+                nc.scalar.activation(picked[:, split:], windows[s][:].indirect(offsets[:, VECTOR_LIST_COLS:]), COPY)
             else:
                 nc.scalar.activation(picked[:], windows[s][:].indirect(offsets[:]), COPY)
             pairs = picked[:].bitcast(F32)
@@ -95,11 +106,11 @@ def tile_list_wgrad_two_batches_pl_kernel(tc, xa, ga, xb, gb, offs, offs2, out_0
             turned[s] = bank
 
         def regroup(s):
+            shape, name = [P, P * PACK], "grouped%d" % s
             if s + 1 in shared:
-                at = (s + 1) * WINDOW_BYTES
-                grouped[s] = laid.tile([P, P * PACK], BF16, name="grouped%d" % s, offset=at, align_bytes=64)
+                grouped[s] = over_window(s + 1, 0, shape, BF16, name)
             else:
-                grouped[s] = keep.tile([P, P * PACK], BF16, name="grouped%d" % s, align_bytes=64)
+                grouped[s] = keep.tile(shape, BF16, name=name, align_bytes=64)
             copy = nc.scalar.copy if s == last_step else nc.vector.tensor_copy
             copy(
                 grouped[s][:].bitcast(F32).rearrange("p (r u) -> p r u", u=2),
@@ -107,84 +118,84 @@ def tile_list_wgrad_two_batches_pl_kernel(tc, xa, ga, xb, gb, offs, offs2, out_0
             )
 
         def quantise(s):
-            if s + 2 in shared or s in (last_step - 2, last_step - 1):
-                at = (s + 2) * WINDOW_BYTES + GROUPED_BYTES
-                if s == last_step - 1:
-                    at = last_step * WINDOW_BYTES
-                codes[s] = laid.tile([P, P], U32, name="codes%d" % s, offset=at, align_bytes=64)
+            shape, name = [P, P], "codes%d" % s
+            if s == last_step - 1:
+                codes[s] = over_window(last_step, 0, shape, U32, name)
+            elif s + 2 in shared or s + 2 == last_step:
+                codes[s] = over_window(s + 2, 1, shape, U32, name)
             else:
-                codes[s] = keep.tile([P, P], U32, name="codes%d" % s, align_bytes=64)
+                codes[s] = keep.tile(shape, U32, name=name, align_bytes=64)
             nc.vector.quantize_mx(codes[s][:].bitcast(steps[s][2]), scales[s][:], grouped[s][:])
 
         def multiply(s):
-            b, batch = divmod(s - 2 * PACK, 2)
+            b, batch = divmod(s - X_STEPS, 2)
             if batch == 0:
                 sums[b] = [sum_psum.tile([P, 2, P], F32, name="sum%d" % h) for h in range(2)]
             for t in range(PACK):
-                x = 2 * t + batch
+                x_step = 2 * t + batch
                 nc.tensor.matmul_mx(
                     sums[b][t // 2][:, t % 2, :],
-                    lhsT=codes[x][:].bitcast(E4M3),
-                    lhsT_scale=scales[x][:],
+                    lhsT=codes[x_step][:].bitcast(E4M3),
+                    lhsT_scale=scales[x_step][:],
                     rhs=codes[s][:].bitcast(steps[s][2]),
                     rhs_scale=scales[s][:],
                     start=(batch == 0 and t % 2 == 0),
                     stop=(batch == 1 and t % 2 == 1),
                 )
 
-        def scale_out(b, h):
-            if h == 0:
-                if b == 1:
-                    at = last_step * WINDOW_BYTES + 2 * GROUPED_BYTES
-                    ys[b] = laid.tile([P, PACK, P], F32, name="y%d" % b, offset=at, align_bytes=64)
-                else:
-                    ys[b] = keep.tile([P, PACK, P], F32, name="y%d" % b, align_bytes=64)
-            half = ys[b][:, 2 * h : 2 * h + 2, :]
-            if b == 0 or (b == BLOCKS - 1 and h == 1):
-                nc.vector.tensor_scalar(half, sums[b][h][:], FACTOR, None, MULT)
+        def scale_out(b):
+            shape, name = [P, PACK, P], "y%d" % b
+            if b == 1:
+                ys[b] = over_window(last_step, 2, shape, F32, name)
             else:
-                nc.scalar.activation(half, sums[b][h][:], COPY, scale=FACTOR)
-            if h == 1:
-                nc.sync.dma_start(y_rows[:, :, b * P : (b + 1) * P], ys[b][:])
+                ys[b] = keep.tile(shape, F32, name=name, align_bytes=64)
+            for h in range(2):
+                half = ys[b][:, 2 * h : 2 * h + 2, :]
+                if b == 0 or (b == last_block and h == 1):
+                    nc.vector.tensor_scalar(half, sums[b][h][:], FACTOR, None, MULT)
+                else:
+                    nc.scalar.activation(half, sums[b][h][:], COPY, scale=FACTOR)
+            nc.sync.dma_start(y_rows[:, :, b * P : (b + 1) * P], ys[b][:])
 
         def round_result(b):
             rounded[b] = keep.tile([P, P * PACK], BF16, name="rounded%d" % b, align_bytes=64)
             target = rounded[b][:].rearrange("p (c i t) -> p c t i", i=4, t=PACK)
             source = ys[b][:].rearrange("p t (c i) -> p c t i", i=4)
-            if b < BLOCKS - 2:
+            if b < last_block - 1:
                 nc.vector.tensor_copy(target, source)
             else:
-                nc.vector.tensor_copy(target[:, :16], source[:, :16])
-                nc.scalar.copy(target[:, 16:], source[:, 16:])
+                middle = P // 4 // 2
+                nc.vector.tensor_copy(target[:, :middle], source[:, :middle])
+                nc.scalar.copy(target[:, middle:], source[:, middle:])
 
         def quantise_result(b):
             cols = slice(b * P, (b + 1) * P)
             nc.vector.quantize_mx(y_codes[:, cols].bitcast(E4M3), y_scales[:, cols], rounded[b][:])
-            if b == BLOCKS - 2:
-                nc.sync.dma_start(word_rows[:, : (b + 1) * P], y_codes[:, : (b + 1) * P].bitcast(I32))
+            if b == EARLY_WORD_BLOCKS - 1:
+                early = slice(0, EARLY_WORD_BLOCKS * P)
+                nc.sync.dma_start(word_rows[:, early], y_codes[:, early].bitcast(I32))
 
         for s in range(AHEAD):
             gather_and_turn(s)
         for s in range(n_steps):
-            done = s // 2 - PACK - 1
             regroup(s)
             quantise(s)
-            if s >= 2 * PACK:
+            if s >= X_STEPS:
                 multiply(s)
             if s + AHEAD < n_steps:
                 gather_and_turn(s + AHEAD)
+            done = (s - X_STEPS) // 2 - 1
             if done >= 0 and s % 2 == 0:
-                scale_out(done, 0)
-                scale_out(done, 1)
+                scale_out(done)
             if done >= 0 and s % 2 == 1:
                 round_result(done)
                 quantise_result(done)
-        scale_out(BLOCKS - 1, 0)
-        scale_out(BLOCKS - 1, 1)
-        round_result(BLOCKS - 1)
-        quantise_result(BLOCKS - 1)
-        last = slice((BLOCKS - 1) * P, BLOCKS * P)
-        nc.sync.dma_start(word_rows[:, last], y_codes[:, last].bitcast(I32))
-        for q in range(4):
+        scale_out(last_block)
+        round_result(last_block)
+        quantise_result(last_block)
+
+        late = slice(EARLY_WORD_BLOCKS * P, BLOCKS * P)
+        nc.sync.dma_start(word_rows[:, late], y_codes[:, late].bitcast(I32))
+        for q in range(QUADRANTS):
             queue = nc.scalar if q % 2 == 0 else nc.sync
             queue.dma_start(scale_rows[4 * q : 4 * q + 4, :], y_scales[32 * q : 32 * q + 4, :].bitcast(I32))

from contextlib import ExitStack

import concourse.mybir as mybir
from concourse.masks import make_identity

F32 = mybir.dt.float32
BF16 = mybir.dt.bfloat16
I32 = mybir.dt.int32
U32 = mybir.dt.uint32
U16 = mybir.dt.uint16
U8 = mybir.dt.uint8
E4M3 = mybir.dt.float8_e4m3fn_x4
E5M2 = mybir.dt.float8_e5m2_x4
COPY = mybir.ActivationFunctionType.Copy
MULT = mybir.AluOpType.mult

P = 128
PACK = 4
TOKENS = 1024
LISTED = 512
ENTRIES_PER_COL = 16
LIST_COLS = LISTED // ENTRIES_PER_COL
BLOCKS = 4
QUADRANTS = 4
FACTOR = 0.04
X_STEPS = 2 * PACK
AHEAD = 4
PICKED_BUFS = 6
SUM_BUFS = 2
VECTOR_LIST_COLS = LIST_COLS // 2
EARLY_WORD_BLOCKS = 2
WINDOW_BYTES = 4 * TOKENS
SLOT_BYTES = 2 * LISTED

FLOPS = 2 * 2 * 512 * 512 * 512


def tile_list_wgrad_two_batches_pl_kernel(tc, xa, ga, xb, gb, offs, offs2, out_0, out_1, out_2):
    nc = tc.nc
    with ExitStack() as ctx:
        keep = ctx.enter_context(tc.tile_pool(name="keep", bufs=1))
        ring = ctx.enter_context(tc.tile_pool(name="ring", bufs=PICKED_BUFS))
        laid = ctx.enter_context(tc.tile_pool(name="laid", bufs=1))
        turn_psum = ctx.enter_context(tc.psum_pool(name="turn_psum", bufs=AHEAD))
        sum_psum = ctx.enter_context(tc.psum_pool(name="sum_psum", bufs=SUM_BUFS))

        def over_window(s, slot, shape, dtype, name):
            at = s * WINDOW_BYTES + slot * SLOT_BYTES
            return laid.tile(shape, dtype, name=name, offset=at, align_bytes=64)

        list_a = keep.tile([P, LIST_COLS], U16, name="list_a")
        list_b = keep.tile([P, LIST_COLS], U16, name="list_b")
        identity = keep.tile([P, P], F32, name="identity")
        make_identity(nc, identity[:])

        xa_rows = xa.rearrange("(m t) c -> t m c", t=PACK)
        xb_rows = xb.rearrange("(m t) c -> t m c", t=PACK)
        steps = []
        for t in range(PACK):
            steps.append((xa_rows[t], list_a, E4M3))
            steps.append((xb_rows[t], list_b, E4M3))
        for b in range(BLOCKS):
            steps.append((ga[b * P : (b + 1) * P, :], list_a, E5M2))
            steps.append((gb[b * P : (b + 1) * P, :], list_b, E4M3))
        n_steps = len(steps)
        last_step = n_steps - 1
        last_block = BLOCKS - 1
        shared = list(range(1, last_step - 3, 2)) + [last_step - 1]

        windows = []
        for s in range(n_steps):
            window = over_window(s, 0, [P, TOKENS], F32, "window%d" % s)
            nc.sync.dma_start(window[:], steps[s][0])
            windows.append(window)
            if s == 0:
                nc.sync.dma_start(list_a[:], offs)
                nc.sync.dma_start(list_b[:], offs2)

        scales = [keep.tile([P, P], U8, name="scales%d" % s, align_bytes=64) for s in range(n_steps)]
        y_codes = keep.tile([P, BLOCKS * P], U32, name="y_codes", align_bytes=64)
        y_scales = keep.tile([P, BLOCKS * P], U8, name="y_scales", align_bytes=64)
        y_rows = out_0.rearrange("(p t) n -> p t n", t=PACK)
        word_rows = out_1[0].rearrange("p n t -> p (n t)").bitcast(I32)
        scale_rows = out_2[0].bitcast(I32)

        turned = {}
        grouped = {}
        codes = {}
        sums = {}
        ys = {}
        rounded = {}

        def gather_and_turn(s):
            picked = ring.tile([P, LISTED], BF16, name="picked", align_bytes=64)
            offsets = steps[s][1]
            if s in shared:
                split = ENTRIES_PER_COL * VECTOR_LIST_COLS
                nc.vector.tensor_copy(picked[:, :split], windows[s][:].indirect(offsets[:, :VECTOR_LIST_COLS]))
                nc.scalar.activation(picked[:, split:], windows[s][:].indirect(offsets[:, VECTOR_LIST_COLS:]), COPY)
            else:
                nc.scalar.activation(picked[:], windows[s][:].indirect(offsets[:]), COPY)
            pairs = picked[:].bitcast(F32)
            bank = turn_psum.tile([P, 2, P], F32, name="bank")
            for u in range(2):
                nc.tensor.transpose(bank[:, u, :], pairs[:, u::2], identity[:])
            turned[s] = bank

        def regroup(s):
            shape, name = [P, P * PACK], "grouped%d" % s
            if s + 1 in shared:
                grouped[s] = over_window(s + 1, 0, shape, BF16, name)
            else:
                grouped[s] = keep.tile(shape, BF16, name=name, align_bytes=64)
            copy = nc.scalar.copy if s == last_step else nc.vector.tensor_copy
            copy(
                grouped[s][:].bitcast(F32).rearrange("p (r u) -> p r u", u=2),
                turned[s][:].rearrange("p u r -> p r u"),
            )

        def quantise(s):
            shape, name = [P, P], "codes%d" % s
            if s == last_step - 1:
                codes[s] = over_window(last_step, 0, shape, U32, name)
            elif s + 2 in shared or s + 2 == last_step:
                codes[s] = over_window(s + 2, 1, shape, U32, name)
            else:
                codes[s] = keep.tile(shape, U32, name=name, align_bytes=64)
            nc.vector.quantize_mx(codes[s][:].bitcast(steps[s][2]), scales[s][:], grouped[s][:])

        def multiply(s):
            b, batch = divmod(s - X_STEPS, 2)
            if batch == 0:
                sums[b] = [sum_psum.tile([P, 2, P], F32, name="sum%d" % h) for h in range(2)]
            for t in range(PACK):
                x_step = 2 * t + batch
                nc.tensor.matmul_mx(
                    sums[b][t // 2][:, t % 2, :],
                    lhsT=codes[x_step][:].bitcast(E4M3),
                    lhsT_scale=scales[x_step][:],
                    rhs=codes[s][:].bitcast(steps[s][2]),
                    rhs_scale=scales[s][:],
                    start=(batch == 0 and t % 2 == 0),
                    stop=(batch == 1 and t % 2 == 1),
                )

        def scale_out(b):
            shape, name = [P, PACK, P], "y%d" % b
            if b == 1:
                ys[b] = over_window(last_step, 2, shape, F32, name)
            else:
                ys[b] = keep.tile(shape, F32, name=name, align_bytes=64)
            for h in range(2):
                half = ys[b][:, 2 * h : 2 * h + 2, :]
                if b == 0 or (b == last_block and h == 1):
                    nc.vector.tensor_scalar(half, sums[b][h][:], FACTOR, None, MULT)
                else:
                    nc.scalar.activation(half, sums[b][h][:], COPY, scale=FACTOR)
            nc.sync.dma_start(y_rows[:, :, b * P : (b + 1) * P], ys[b][:])

        def round_result(b):
            rounded[b] = keep.tile([P, P * PACK], BF16, name="rounded%d" % b, align_bytes=64)
            target = rounded[b][:].rearrange("p (c i t) -> p c t i", i=4, t=PACK)
            source = ys[b][:].rearrange("p t (c i) -> p c t i", i=4)
            if b < last_block - 1:
                nc.vector.tensor_copy(target, source)
            else:
                middle = P // 4 // 2
                nc.vector.tensor_copy(target[:, :middle], source[:, :middle])
                nc.scalar.copy(target[:, middle:], source[:, middle:])

        def quantise_result(b):
            cols = slice(b * P, (b + 1) * P)
            nc.vector.quantize_mx(y_codes[:, cols].bitcast(E4M3), y_scales[:, cols], rounded[b][:])
            if b == EARLY_WORD_BLOCKS - 1:
                early = slice(0, EARLY_WORD_BLOCKS * P)
                nc.sync.dma_start(word_rows[:, early], y_codes[:, early].bitcast(I32))

        for s in range(AHEAD):
            gather_and_turn(s)
        for s in range(n_steps):
            regroup(s)
            quantise(s)
            if s >= X_STEPS:
                multiply(s)
            if s + AHEAD < n_steps:
                gather_and_turn(s + AHEAD)
            done = (s - X_STEPS) // 2 - 1
            if done >= 0 and s % 2 == 0:
                scale_out(done)
            if done >= 0 and s % 2 == 1:
                round_result(done)
                quantise_result(done)
        scale_out(last_block)
        round_result(last_block)
        quantise_result(last_block)

        late = slice(EARLY_WORD_BLOCKS * P, BLOCKS * P)
        nc.sync.dma_start(word_rows[:, late], y_codes[:, late].bitcast(I32))
        for q in range(QUADRANTS):
            queue = nc.scalar if q % 2 == 0 else nc.sync
            queue.dma_start(scale_rows[4 * q : 4 * q + 4, :], y_scales[32 * q : 32 * q + 4, :].bitcast(I32))
